import numpy as np, ml_dtypes
CORES = [118,246,374,502,126,254,382,510]
N = 8
G1 = [0,1,2,3,4,5,6,7]
G2 = [0,2,4,6]
G3 = [1,3,5,7]
ROOT3 = 0
def setup_inputs(rng):
    return {"x1": rng.standard_normal((N, 128, 512), dtype=np.float32), "x2": rng.standard_normal((N, 128, 8), dtype=np.float32), "x3": rng.standard_normal((N, 128, 256), dtype=np.float32).astype(ml_dtypes.bfloat16)}
def reference(x1, x2, x3):
    out = {}
    y = np.full((N, 128, 64), np.nan, x1.dtype)
    s = x1[G1].sum(axis=0, dtype=np.float64).astype(x1.dtype)
    for i, r in enumerate(G1):
        y[r] = s[:, 64 * i:64 * i + 64]
    out["y1"] = y
    y = np.full((N, 128, 8), np.nan, x2.dtype)
    for i, r in enumerate(G2):
        y[r] = np.concatenate([x2[s][:, 2 * i:2 * i + 2] for s in G2], axis=1)
    out["y2"] = y
    y = np.full((N, 128, 1024), np.nan, x3.dtype)
    y[G3[ROOT3]] = np.concatenate([x3[r] for r in G3], axis=1)
    out["y3"] = y
    return out

@@ -1,0 +1,207 @@
+from concourse.bass import DstId, RemoteDMATransfer
+from concourse.mybir import AluOpType
+
+SCRATCH = {
+    "xs": ("dram", [7, 128, 64], "float32"),
+    "m1": ("dram", [4, 128, 64], "float32"),
+    "m2": ("dram", [2, 128, 64], "float32"),
+    "m3": ("dram", [128, 64], "float32"),
+    "a2s": ("dram", [128, 8], "float32"),
+    "a2l": ("dram", [4, 128, 8], "float32"),
+    "g3s": ("dram", [128, 256], "bfloat16"),
+    "g3l": ("dram", [3, 128, 256], "bfloat16"),
+}
+SEMAPHORES = ["L0", "L1", "L2", "L3", "L4", "L5", "L6", "LX", "yc", "ysem",
+              "A1a", "A1b", "A1c", "A1x", "A2a", "A2b", "A3", "sent", "fin",
+              "a2r", "a2a0", "a2a1", "a2a2", "a2a3", "g3r", "g3a0", "g3a1", "g3a2"]
+
+A2_RELAY_CORE = 4
+G3_RELAY_SAME = 5
+G3_RELAY_CROSS = 2
+
+
+def _wc(h, ch, k):
+    return h * 128 + ch * 8 + k
+
+
+def _bits(m):
+    return bin(m).count("1")
+
+
+def rank_program(g, core, T, topo):
+    S = T.sem
+    cores = list(T.cores)
+    G1, G2, G3, root3 = T.tables["G1"], T.tables["G2"], T.tables["G3"], T.tables["ROOT3"]
+    H, C = topo.host, topo.chip
+    at = {}
+    for r, c in enumerate(cores):
+        at[(H(c), C(c))] = r
+    sent = [0]
+
+    def tr(dst_core, dst_ap, srcs, sem, mask):
+        rid, pid = topo.addr(dst_core, core)
+        sent[0] += _bits(mask)
+        if len(srcs) == 1:
+            return RemoteDMATransfer(dst_ids=[DstId(rid=rid, pnc=pid)], dma_engine_mask=mask, remote_sem=sem,
+                                     src=srcs[0], dst=dst_ap, alu_op=0)
+        return RemoteDMATransfer(dst_ids=[DstId(rid=rid, pnc=pid)], dma_engine_mask=mask, remote_sem=sem,
+                                 srcs=list(srcs), dsts=[dst_ap], alu_op=1)
+
+    def fused(transfers):
+        g.remote_dma_fused(transfers, local_sem=S.sent)
+
+    def copy(dst_core, dst_ap, src_ap, sem, mask=0xFF):
+        rid, pid = topo.addr(dst_core, core)
+        sent[0] += _bits(mask)
+        g.remote_dma(dst_ap, src_ap, sem, S.sent, pid, rid, mask)
+
+    M_DIRECT, M_SAME, M_CROSS = 0xC0, 0x30, 0x0F
+    a2_out = {}
+    a2_relay = {}
+    for j, rs in enumerate(G2):
+        cs = cores[rs]
+        for i, rd in enumerate(G2):
+            if i == j:
+                continue
+            cd = cores[rd]
+            if H(cs) == H(cd):
+                a2_out.setdefault(cs, []).append((cd, j, M_DIRECT, False))
+            else:
+                rel = _wc(H(cs) ^ 1, C(cd), A2_RELAY_CORE)
+                a2_out.setdefault(cs, []).append((rel, j, M_SAME if C(cs) == C(cd) else M_CROSS, True))
+                a2_relay.setdefault(rel, []).append((j, cd))
+    root = cores[G3[root3]]
+    g3_slot = {}
+    g3_first = {}
+    g3_relay = {}
+    for j, rs in enumerate(G3):
+        if j == root3:
+            continue
+        k = len(g3_slot)
+        g3_slot[j] = k
+        cs = cores[rs]
+        if H(cs) == H(root):
+            g3_first[cs] = (root, k, True)
+        else:
+            if C(cs) == C(root):
+                rel = _wc(H(cs) ^ 1, C(cs), G3_RELAY_SAME)
+            else:
+                rel = _wc(3 - H(cs), C(cs), G3_RELAY_CROSS)
+            g3_first[cs] = (rel, k, False)
+            g3_relay[rel] = k
+
+    rank = T.rank_of(core)
+    if rank is None:
+        if core in a2_relay:
+            g.wait_ge(S.a2r, _bits(M_SAME) + _bits(M_CROSS))
+            masks = [0x0F, 0xF0]
+            fused([tr(cd, T.a2l[j], [T.a2l[j]], S["a2a%d" % j], masks[n])
+                   for n, (j, cd) in enumerate(a2_relay[core])])
+            g.wait_ge(S.sent, sent[0])
+        if core in g3_relay:
+            k = g3_relay[core]
+            g.wait_ge(S.g3r, 8)
+            copy(root, T.g3l[k], T.g3s[:, :], S["g3a%d" % k])
+            g.wait_ge(S.sent, sent[0])
+        return
+
+    h, ch = H(core), C(core)
+    oc, sw, cb, dg = ch ^ 1, h ^ 1, 3 - h, (h + 2) % 4
+    mate, swp, cbp, xsw = cores[at[(h, oc)]], cores[at[(sw, ch)]], cores[at[(cb, ch)]], cores[at[(sw, oc)]]
+
+    def cols(hh, cc):
+        a = 64 * G1.index(at[(hh, cc)])
+        return T.x1[:, a:a + 64]
+
+    slot_chunk = [(dg, oc), (cb, oc), (sw, oc), (h, oc), (dg, ch), (sw, ch), (cb, ch)]
+    in2, in3 = rank in G2, rank in G3
+    fin = [0]
+
+    def load(q, k):
+        q.dma_start(T.xs[k], cols(*slot_chunk[k])).then_inc(S["L%d" % k], 16)
+
+    def last(q, out, in_):
+        q.dma_start(out, in_).then_inc(S.fin, 16)
+        fin[0] += 16
+
+    load(g.sync, 0)
+    if in2:
+        g.scalar.dma_start(T.a2s[:, :], T.x2[:, :]).then_inc(S.LX, 16)
+    elif core in g3_first:
+        g.scalar.dma_start(T.g3s[:, :], T.x3[:, :]).then_inc(S.LX, 16)
+    load(g.scalar, 1)
+    load(g.sync, 2)
+    load(g.sync, 3)
+    load(g.scalar, 4)
+    load(g.scalar, 5)
+    load(g.sync, 6)
+    g.scalar.dma_start(T.y1[:, :], cols(h, ch)).then_inc(S.yc, 16)
+
+    if in2:
+        i = G2.index(rank)
+        last(g.scalar, T.y2[:, 2 * i:2 * i + 2], T.x2[:, 2 * i:2 * i + 2])
+        far = []
+        for j, rs in enumerate(G2):
+            if j == i:
+                continue
+            if H(cores[rs]) == h:
+                g.sync.wait_ge(S["a2a%d" % j], _bits(M_DIRECT))
+                last(g.sync, T.y2[:, 2 * j:2 * j + 2], T.a2l[j, :, 2 * i:2 * i + 2])
+            else:
+                far.append(j)
+        for q, j in zip([g.sync, g.scalar], far):
+            q.wait_ge(S["a2a%d" % j], 4)
+            last(q, T.y2[:, 2 * j:2 * j + 2], T.a2l[j, :, 2 * i:2 * i + 2])
+    if core == root:
+        last(g.scalar, T.y3[:, 256 * root3:256 * root3 + 256], T.x3[:, :])
+        near = [j for j in g3_slot if H(cores[G3[j]]) == h]
+        far = [j for j in g3_slot if H(cores[G3[j]]) != h]
+        for q, j in zip([g.sync, g.scalar, g.sync], near + far):
+            q.wait_ge(S["g3a%d" % g3_slot[j]], 8)
+            last(q, T.y3[:, 256 * j:256 * j + 256], T.g3l[g3_slot[j]])
+
+    def g3_send():
+        tgt, k, direct = g3_first[core]
+        g.wait_ge(S.LX, 16)
+        if direct:
+            copy(tgt, T.g3l[k], T.g3s[:, :], S["g3a%d" % k])
+        else:
+            copy(tgt, T.g3s[:, :], T.g3s[:, :], S.g3r)
+
+    g.wait_ge(S.L0, 16)
+    copy(mate, T.m1[0], T.xs[0], S.A1a)
+    if core in g3_first and not g3_first[core][2]:
+        g3_send()
+    g.wait_ge(S.L1, 16)
+    g.wait_ge(S.L2, 16)
+    g.wait_ge(S.L3, 16)
+    fused([tr(xsw, T.m1[3], [T.xs[3]], S.A1x, 0x0F),
+           tr(mate, T.m1[2], [T.xs[2]], S.A1c, 0x30),
+           tr(mate, T.m1[1], [T.xs[1]], S.A1b, 0xC0)])
+    if in2:
+        g.wait_ge(S.LX, 16)
+        fused([tr(tgt, T.a2l[j], [T.a2s[:, :]], S.a2r if rel else S["a2a%d" % j], m)
+               for (tgt, j, m, rel) in a2_out[core]])
+    g.wait_ge(S.A1a, 8)
+    g.wait_ge(S.L4, 16)
+    fused([tr(swp, T.m2[0], [T.xs[4], T.m1[0]], S.A2a, 0xFF)])
+    g.wait_ge(S.A1c, 2)
+    g.wait_ge(S.A1x, 4)
+    g.wait_ge(S.L5, 16)
+    fused([tr(swp, T.m2[1], [T.xs[5], T.m1[2], T.m1[3]], S.A2b, 0xFF)])
+    if core in g3_first and g3_first[core][2]:
+        g3_send()
+    g.wait_ge(S.A2a, 8)
+    g.wait_ge(S.A1b, 2)
+    g.wait_ge(S.L6, 16)
+    fused([tr(cbp, T.m3[:, :], [T.xs[6], T.m1[1], T.m2[0]], S.A3, 0xFF)])
+    g.wait_ge(S.A2b, 8)
+    g.wait_ge(S.yc, 16)
+    g.dma_start(T.y1[:, :], T.m2[1], accum_op=AluOpType.add, max_dma_last_dim=8192).then_inc(S.ysem, 16)
+    g.wait_ge(S.A3, 8)
+    g.wait_ge(S.ysem, 16)
+    g.dma_start(T.y1[:, :], T.m3[:, :], accum_op=AluOpType.add, max_dma_last_dim=8192).then_inc(S.ysem, 16)
+    g.wait_ge(S.ysem, 32)
+    g.wait_ge(S.sent, sent[0])
+    if fin[0]:
+        g.wait_ge(S.fin, fin[0])

@@ -2,22 +2,25 @@ from concourse.bass import DstId, RemoteDMATransfer
 from concourse.mybir import AluOpType
 
 SCRATCH = {
-    "xs": ("dram", [7, 128, 64], "float32"),
-    "m1": ("dram", [4, 128, 64], "float32"),
-    "m2": ("dram", [2, 128, 64], "float32"),
+    "xs": ("dram", [8, 128, 64], "float32"),
+    "m1": ("dram", [2, 128, 64], "float32"),
+    "m2": ("dram", [128, 64], "float32"),
     "m3": ("dram", [128, 64], "float32"),
+    "hA": ("dram", [4, 128, 64], "float32"),
+    "mA": ("dram", [128, 64], "float32"),
     "a2s": ("dram", [128, 8], "float32"),
     "a2l": ("dram", [4, 128, 8], "float32"),
-    "g3s": ("dram", [128, 256], "bfloat16"),
-    "g3l": ("dram", [3, 128, 256], "bfloat16"),
+    "g3s": ("dram", [2, 128, 128], "bfloat16"),
+    "g3l": ("dram", [6, 128, 128], "bfloat16"),
 }
-SEMAPHORES = ["L0", "L1", "L2", "L3", "L4", "L5", "L6", "LX", "yc", "ysem",
-              "A1a", "A1b", "A1c", "A1x", "A2a", "A2b", "A3", "sent", "fin",
-              "a2r", "a2a0", "a2a1", "a2a2", "a2a3", "g3r", "g3a0", "g3a1", "g3a2"]
+SEMAPHORES = ["L0", "L1", "L2", "L3", "L4", "L5", "L6", "L7", "LX", "yc", "ysem",
+              "A1a", "A1b", "A2", "A3", "hAs", "AA", "sent", "fin",
+              "a2r", "a2a0", "a2a1", "a2a2", "a2a3", "g3r", "g3a0", "g3a1", "g3a2", "g3a3", "g3a4", "g3a5"]
 
+A_FOLD_CORE = 7
 A2_RELAY_CORE = 4
-G3_RELAY_SAME = 5
-G3_RELAY_CROSS = 2
+G3_RELAY_SW = (5, 2)
+G3_RELAY_CB = (0, 2)
 
 
 def _wc(h, ch, k):
@@ -77,21 +80,26 @@ def rank_program(g, core, T, topo):
     for j, rs in enumerate(G3):
         if j == root3:
             continue
-        k = len(g3_slot)
+        k = 2 * len(g3_slot)
         g3_slot[j] = k
         cs = cores[rs]
         if H(cs) == H(root):
-            g3_first[cs] = (root, k, True)
+            g3_first[cs] = ([(root, 0, k), (root, 1, k + 1)], True)
         else:
-            if C(cs) == C(root):
-                rel = _wc(H(cs) ^ 1, C(cs), G3_RELAY_SAME)
-            else:
-                rel = _wc(3 - H(cs), C(cs), G3_RELAY_CROSS)
-            g3_first[cs] = (rel, k, False)
-            g3_relay[rel] = k
+            x = 0 if C(cs) == C(root) else 1
+            r0 = _wc(H(cs) ^ 1, C(root), G3_RELAY_SW[x])
+            r1 = _wc(3 - H(cs), C(cs), G3_RELAY_CB[x])
+            g3_first[cs] = ([(r0, 0, k), (r1, 1, k + 1)], False)
+            g3_relay[r0] = (0, k)
+            g3_relay[r1] = (1, k + 1)
 
+    MA_ON, MA_CROSS, MA_MATE, MA_SW = 0xFF00, 0x000F, 0x0030, 0x00C0
     rank = T.rank_of(core)
     if rank is None:
+        if core % 8 == A_FOLD_CORE and (H(core), C(core)) in at:
+            g.wait_ge(S.hAs, 16)
+            fused([tr(cores[at[(H(core), C(core))]], T.mA[:, :], [T.hA[0], T.hA[1], T.hA[2], T.hA[3]], S.AA, 0xFFFF)])
+            g.wait_ge(S.sent, sent[0])
         if core in a2_relay:
             g.wait_ge(S.a2r, _bits(M_SAME) + _bits(M_CROSS))
             masks = [0x0F, 0xF0]
@@ -99,22 +107,22 @@ def rank_program(g, core, T, topo):
                    for n, (j, cd) in enumerate(a2_relay[core])])
             g.wait_ge(S.sent, sent[0])
         if core in g3_relay:
-            k = g3_relay[core]
-            g.wait_ge(S.g3r, 8)
-            copy(root, T.g3l[k], T.g3s[:, :], S["g3a%d" % k])
+            t, k = g3_relay[core]
+            g.wait_ge(S.g3r, 4)
+            copy(root, T.g3l[k], T.g3s[t], S["g3a%d" % k])
             g.wait_ge(S.sent, sent[0])
         return
 
     h, ch = H(core), C(core)
     oc, sw, cb, dg = ch ^ 1, h ^ 1, 3 - h, (h + 2) % 4
-    mate, swp, cbp, xsw = cores[at[(h, oc)]], cores[at[(sw, ch)]], cores[at[(cb, ch)]], cores[at[(sw, oc)]]
+    mate, swp, cbp = cores[at[(h, oc)]], cores[at[(sw, ch)]], cores[at[(cb, ch)]]
 
     def cols(hh, cc):
         a = 64 * G1.index(at[(hh, cc)])
         return T.x1[:, a:a + 64]
 
-    slot_chunk = [(dg, oc), (cb, oc), (sw, oc), (h, oc), (dg, ch), (sw, ch), (cb, ch)]
-    in2, in3 = rank in G2, rank in G3
+    slot_chunk = [(dg, oc), (cb, oc), (sw, oc), (h, oc), (dg, ch), (sw, ch), (cb, ch), (h, ch)]
+    in2 = rank in G2
     fin = [0]
 
     def load(q, k):
@@ -128,14 +136,16 @@ def rank_program(g, core, T, topo):
     if in2:
         g.scalar.dma_start(T.a2s[:, :], T.x2[:, :]).then_inc(S.LX, 16)
     elif core in g3_first:
-        g.scalar.dma_start(T.g3s[:, :], T.x3[:, :]).then_inc(S.LX, 16)
-    load(g.scalar, 1)
-    load(g.sync, 2)
+        g.scalar.dma_start(T.g3s[:, :, :], T.x3[:, :]).then_inc(S.LX, 16)
+    load(g.scalar, 2)
     load(g.sync, 3)
-    load(g.scalar, 4)
     load(g.scalar, 5)
+    load(g.sync, 7)
+    load(g.scalar, 1)
+    load(g.sync, 4)
     load(g.sync, 6)
-    g.scalar.dma_start(T.y1[:, :], cols(h, ch)).then_inc(S.yc, 16)
+    g.sync.wait_ge(S.AA, 16)
+    g.sync.dma_start(T.y1[:, :], T.mA[:, :]).then_inc(S.yc, 16)
 
     if in2:
         i = G2.index(rank)
@@ -145,63 +155,61 @@ def rank_program(g, core, T, topo):
             if j == i:
                 continue
             if H(cores[rs]) == h:
-                g.sync.wait_ge(S["a2a%d" % j], _bits(M_DIRECT))
-                last(g.sync, T.y2[:, 2 * j:2 * j + 2], T.a2l[j, :, 2 * i:2 * i + 2])
+                g.scalar.wait_ge(S["a2a%d" % j], _bits(M_DIRECT))
+                last(g.scalar, T.y2[:, 2 * j:2 * j + 2], T.a2l[j, :, 2 * i:2 * i + 2])
             else:
                 far.append(j)
-        for q, j in zip([g.sync, g.scalar], far):
+        for q, j in zip([g.scalar, g.sync], far):
             q.wait_ge(S["a2a%d" % j], 4)
             last(q, T.y2[:, 2 * j:2 * j + 2], T.a2l[j, :, 2 * i:2 * i + 2])
     if core == root:
         last(g.scalar, T.y3[:, 256 * root3:256 * root3 + 256], T.x3[:, :])
         near = [j for j in g3_slot if H(cores[G3[j]]) == h]
         far = [j for j in g3_slot if H(cores[G3[j]]) != h]
-        for q, j in zip([g.sync, g.scalar, g.sync], near + far):
-            q.wait_ge(S["g3a%d" % g3_slot[j]], 8)
-            last(q, T.y3[:, 256 * j:256 * j + 256], T.g3l[g3_slot[j]])
+        for t, q in enumerate([g.scalar, g.sync]):
+            for j in far:
+                q.wait_ge(S["g3a%d" % (g3_slot[j] + t)], 8)
+                last(q, T.y3[64 * t:64 * t + 64, 256 * j:256 * j + 256], T.g3l[g3_slot[j] + t])
+        for j in near:
+            k = g3_slot[j]
+            g.scalar.wait_ge(S["g3a%d" % k], 8)
+            last(g.scalar, T.y3[:, 256 * j:256 * j + 256], T.g3l[k:k + 2])
 
     def g3_send():
-        tgt, k, direct = g3_first[core]
+        legs, direct = g3_first[core]
         g.wait_ge(S.LX, 16)
-        if direct:
-            copy(tgt, T.g3l[k], T.g3s[:, :], S["g3a%d" % k])
-        else:
-            copy(tgt, T.g3s[:, :], T.g3s[:, :], S.g3r)
+        fused([tr(tgt, T.g3l[k] if direct else T.g3s[t], [T.g3s[t]], S["g3a%d" % legs[0][2]] if direct else S.g3r,
+                  (0x0F, 0xF0)[t]) for (tgt, t, k) in legs])
 
     g.wait_ge(S.L0, 16)
     copy(mate, T.m1[0], T.xs[0], S.A1a)
-    if core in g3_first and not g3_first[core][2]:
+    if core in g3_first and not g3_first[core][1]:
         g3_send()
-    g.wait_ge(S.L1, 16)
-    g.wait_ge(S.L2, 16)
-    g.wait_ge(S.L3, 16)
-    fused([tr(xsw, T.m1[3], [T.xs[3]], S.A1x, 0x0F),
-           tr(mate, T.m1[2], [T.xs[2]], S.A1c, 0x30),
-           tr(mate, T.m1[1], [T.xs[1]], S.A1b, 0xC0)])
     if in2:
         g.wait_ge(S.LX, 16)
         fused([tr(tgt, T.a2l[j], [T.a2s[:, :]], S.a2r if rel else S["a2a%d" % j], m)
                for (tgt, j, m, rel) in a2_out[core]])
+    for k in (2, 3, 5, 7):
+        g.wait_ge(S["L%d" % k], 16)
+    fused([tr(_wc(sw, oc, A_FOLD_CORE), T.hA[3], [T.xs[2]], S.hAs, MA_CROSS),
+           tr(_wc(h, oc, A_FOLD_CORE), T.hA[1], [T.xs[3]], S.hAs, MA_MATE),
+           tr(_wc(sw, ch, A_FOLD_CORE), T.hA[2], [T.xs[5]], S.hAs, MA_SW),
+           tr(_wc(h, ch, A_FOLD_CORE), T.hA[0], [T.xs[7]], S.hAs, MA_ON)])
+    g.wait_ge(S.L1, 16)
+    copy(mate, T.m1[1], T.xs[1], S.A1b)
+    if core in g3_first and g3_first[core][1]:
+        g3_send()
     g.wait_ge(S.A1a, 8)
     g.wait_ge(S.L4, 16)
-    fused([tr(swp, T.m2[0], [T.xs[4], T.m1[0]], S.A2a, 0xFF)])
-    g.wait_ge(S.A1c, 2)
-    g.wait_ge(S.A1x, 4)
-    g.wait_ge(S.L5, 16)
-    fused([tr(swp, T.m2[1], [T.xs[5], T.m1[2], T.m1[3]], S.A2b, 0xFF)])
-    if core in g3_first and g3_first[core][2]:
-        g3_send()
-    g.wait_ge(S.A2a, 8)
-    g.wait_ge(S.A1b, 2)
+    fused([tr(swp, T.m2[:, :], [T.xs[4], T.m1[0]], S.A2, 0xFF)])
+    g.wait_ge(S.A2, 8)
+    g.wait_ge(S.A1b, 8)
     g.wait_ge(S.L6, 16)
-    fused([tr(cbp, T.m3[:, :], [T.xs[6], T.m1[1], T.m2[0]], S.A3, 0xFF)])
-    g.wait_ge(S.A2b, 8)
-    g.wait_ge(S.yc, 16)
-    g.dma_start(T.y1[:, :], T.m2[1], accum_op=AluOpType.add, max_dma_last_dim=8192).then_inc(S.ysem, 16)
+    fused([tr(cbp, T.m3[:, :], [T.xs[6], T.m1[1], T.m2[:, :]], S.A3, 0xFF)])
     g.wait_ge(S.A3, 8)
-    g.wait_ge(S.ysem, 16)
+    g.wait_ge(S.yc, 16)
     g.dma_start(T.y1[:, :], T.m3[:, :], accum_op=AluOpType.add, max_dma_last_dim=8192).then_inc(S.ysem, 16)
-    g.wait_ge(S.ysem, 32)
+    g.wait_ge(S.ysem, 16)
     g.wait_ge(S.sent, sent[0])
     if fin[0]:
         g.wait_ge(S.fin, fin[0])

@@ -21,6 +21,7 @@ A_FOLD_CORE = 7
 A2_RELAY_CORE = 4
 G3_RELAY_SW = (5, 2)
 G3_RELAY_CB = (0, 2)
+G3_RELAY_MATE = (2, 3)
 
 
 def _wc(h, ch, k):
@@ -84,14 +85,16 @@ def rank_program(g, core, T, topo):
         g3_slot[j] = k
         cs = cores[rs]
         if H(cs) == H(root):
-            g3_first[cs] = ([(root, 0, k), (root, 1, k + 1)], True)
+            r0 = _wc(H(cs), C(cs), G3_RELAY_MATE[0])
+            r1 = _wc(H(cs), C(cs), G3_RELAY_MATE[1])
+            g3_first[cs] = [(r0, 0, 0x0F00), (r1, 1, 0xF000)]
         else:
             x = 0 if C(cs) == C(root) else 1
-            r0 = _wc(H(cs) ^ 1, C(root), G3_RELAY_SW[x])
+            r0 = _wc(H(cs) ^ 1, C(cs), G3_RELAY_SW[x])
             r1 = _wc(3 - H(cs), C(cs), G3_RELAY_CB[x])
-            g3_first[cs] = ([(r0, 0, k), (r1, 1, k + 1)], False)
-            g3_relay[r0] = (0, k)
-            g3_relay[r1] = (1, k + 1)
+            g3_first[cs] = [(r0, 0, 0x000F), (r1, 1, 0x00F0)]
+        g3_relay[r0] = (0, k)
+        g3_relay[r1] = (1, k + 1)
 
     MA_ON, MA_CROSS, MA_MATE, MA_SW = 0xFF00, 0x000F, 0x0030, 0x00C0
     rank = T.rank_of(core)
@@ -137,12 +140,12 @@ def rank_program(g, core, T, topo):
         g.scalar.dma_start(T.a2s[:, :], T.x2[:, :]).then_inc(S.LX, 16)
     elif core in g3_first:
         g.scalar.dma_start(T.g3s[:, :, :], T.x3[:, :]).then_inc(S.LX, 16)
+    load(g.scalar, 1)
+    load(g.sync, 4)
     load(g.scalar, 2)
     load(g.sync, 3)
     load(g.scalar, 5)
     load(g.sync, 7)
-    load(g.scalar, 1)
-    load(g.sync, 4)
     load(g.sync, 6)
     g.sync.wait_ge(S.AA, 16)
     g.sync.dma_start(T.y1[:, :], T.mA[:, :]).then_inc(S.yc, 16)
@@ -167,41 +170,30 @@ def rank_program(g, core, T, topo):
         near = [j for j in g3_slot if H(cores[G3[j]]) == h]
         far = [j for j in g3_slot if H(cores[G3[j]]) != h]
         for t, q in enumerate([g.scalar, g.sync]):
-            for j in far:
+            for j in near + far:
                 q.wait_ge(S["g3a%d" % (g3_slot[j] + t)], 8)
                 last(q, T.y3[64 * t:64 * t + 64, 256 * j:256 * j + 256], T.g3l[g3_slot[j] + t])
-        for j in near:
-            k = g3_slot[j]
-            g.scalar.wait_ge(S["g3a%d" % k], 8)
-            last(g.scalar, T.y3[:, 256 * j:256 * j + 256], T.g3l[k:k + 2])
-
-    def g3_send():
-        legs, direct = g3_first[core]
-        g.wait_ge(S.LX, 16)
-        fused([tr(tgt, T.g3l[k] if direct else T.g3s[t], [T.g3s[t]], S["g3a%d" % legs[0][2]] if direct else S.g3r,
-                  (0x0F, 0xF0)[t]) for (tgt, t, k) in legs])
 
     g.wait_ge(S.L0, 16)
     copy(mate, T.m1[0], T.xs[0], S.A1a)
-    if core in g3_first and not g3_first[core][1]:
-        g3_send()
+    if core in g3_first:
+        g.wait_ge(S.LX, 16)
+        fused([tr(tgt, T.g3s[t], [T.g3s[t]], S.g3r, m) for (tgt, t, m) in g3_first[core]])
     if in2:
         g.wait_ge(S.LX, 16)
         fused([tr(tgt, T.a2l[j], [T.a2s[:, :]], S.a2r if rel else S["a2a%d" % j], m)
                for (tgt, j, m, rel) in a2_out[core]])
+    g.wait_ge(S.L1, 16)
+    copy(mate, T.m1[1], T.xs[1], S.A1b)
+    g.wait_ge(S.A1a, 8)
+    g.wait_ge(S.L4, 16)
+    fused([tr(swp, T.m2[:, :], [T.xs[4], T.m1[0]], S.A2, 0xFF)])
     for k in (2, 3, 5, 7):
         g.wait_ge(S["L%d" % k], 16)
     fused([tr(_wc(sw, oc, A_FOLD_CORE), T.hA[3], [T.xs[2]], S.hAs, MA_CROSS),
            tr(_wc(h, oc, A_FOLD_CORE), T.hA[1], [T.xs[3]], S.hAs, MA_MATE),
            tr(_wc(sw, ch, A_FOLD_CORE), T.hA[2], [T.xs[5]], S.hAs, MA_SW),
            tr(_wc(h, ch, A_FOLD_CORE), T.hA[0], [T.xs[7]], S.hAs, MA_ON)])
-    g.wait_ge(S.L1, 16)
-    copy(mate, T.m1[1], T.xs[1], S.A1b)
-    if core in g3_first and g3_first[core][1]:
-        g3_send()
-    g.wait_ge(S.A1a, 8)
-    g.wait_ge(S.L4, 16)
-    fused([tr(swp, T.m2[:, :], [T.xs[4], T.m1[0]], S.A2, 0xFF)])
     g.wait_ge(S.A2, 8)
     g.wait_ge(S.A1b, 8)
     g.wait_ge(S.L6, 16)

from concourse.bass import DstId, RemoteDMATransfer
from concourse.mybir import AluOpType

SCRATCH = {
    "xs": ("dram", [8, 128, 64], "float32"),
    "m1": ("dram", [2, 128, 64], "float32"),
    "m2": ("dram", [128, 64], "float32"),
    "m3": ("dram", [128, 64], "float32"),
    "hA": ("dram", [4, 128, 64], "float32"),
    "mA": ("dram", [128, 64], "float32"),
    "a2s": ("dram", [128, 8], "float32"),
    "a2l": ("dram", [4, 128, 8], "float32"),
    "g3s": ("dram", [2, 128, 128], "bfloat16"),
    "g3l": ("dram", [6, 128, 128], "bfloat16"),
}
SEMAPHORES = ["L0", "L1", "L2", "L3", "L4", "L5", "L6", "L7", "LX", "yc", "ysem",
              "A1a", "A1b", "A2", "A3", "hAs", "AA", "sent", "fin",
              "a2r", "a2a0", "a2a1", "a2a2", "a2a3", "g3r", "g3a0", "g3a1", "g3a2", "g3a3", "g3a4", "g3a5"]

A_FOLD_CORE = 7
A2_RELAY_CORE = 4
G3_RELAY_SW = (5, 2)
G3_RELAY_CB = (0, 2)
G3_RELAY_MATE = (2, 3)


def _wc(h, ch, k):
    return h * 128 + ch * 8 + k


def _bits(m):
    return bin(m).count("1")


def rank_program(g, core, T, topo):
    S = T.sem
    cores = list(T.cores)
    G1, G2, G3, root3 = T.tables["G1"], T.tables["G2"], T.tables["G3"], T.tables["ROOT3"]
    H, C = topo.host, topo.chip
    at = {}
    for r, c in enumerate(cores):
        at[(H(c), C(c))] = r
    sent = [0]

    def tr(dst_core, dst_ap, srcs, sem, mask):
        rid, pid = topo.addr(dst_core, core)
        sent[0] += _bits(mask)
        if len(srcs) == 1:
            return RemoteDMATransfer(dst_ids=[DstId(rid=rid, pnc=pid)], dma_engine_mask=mask, remote_sem=sem,
                                     src=srcs[0], dst=dst_ap, alu_op=0)
        return RemoteDMATransfer(dst_ids=[DstId(rid=rid, pnc=pid)], dma_engine_mask=mask, remote_sem=sem,
                                 srcs=list(srcs), dsts=[dst_ap], alu_op=1)

    def fused(transfers):
        g.remote_dma_fused(transfers, local_sem=S.sent)

    def copy(dst_core, dst_ap, src_ap, sem, mask=0xFF):
        rid, pid = topo.addr(dst_core, core)
        sent[0] += _bits(mask)
        g.remote_dma(dst_ap, src_ap, sem, S.sent, pid, rid, mask)

    M_DIRECT, M_SAME, M_CROSS = 0xC0, 0x30, 0x0F
    a2_out = {}
    a2_relay = {}
    for j, rs in enumerate(G2):
        cs = cores[rs]
        for i, rd in enumerate(G2):
            if i == j:
                continue
            cd = cores[rd]
            if H(cs) == H(cd):
                a2_out.setdefault(cs, []).append((cd, j, M_DIRECT, False))
            else:
                rel = _wc(H(cs) ^ 1, C(cd), A2_RELAY_CORE)
                a2_out.setdefault(cs, []).append((rel, j, M_SAME if C(cs) == C(cd) else M_CROSS, True))
                a2_relay.setdefault(rel, []).append((j, cd))
    root = cores[G3[root3]]
    g3_slot = {}
    g3_first = {}
    g3_relay = {}
    for j, rs in enumerate(G3):
        if j == root3:
            continue
        k = 2 * len(g3_slot)
        g3_slot[j] = k
        cs = cores[rs]
        if H(cs) == H(root):
            r0 = _wc(H(cs), C(cs), G3_RELAY_MATE[0])
            r1 = _wc(H(cs), C(cs), G3_RELAY_MATE[1])
            g3_first[cs] = [(r0, 0, 0x0F00), (r1, 1, 0xF000)]
        else:
            x = 0 if C(cs) == C(root) else 1
            r0 = _wc(H(cs) ^ 1, C(cs), G3_RELAY_SW[x])
            r1 = _wc(3 - H(cs), C(cs), G3_RELAY_CB[x])
            g3_first[cs] = [(r0, 0, 0x000F), (r1, 1, 0x00F0)]
        g3_relay[r0] = (0, k)
        g3_relay[r1] = (1, k + 1)

    MA_ON, MA_CROSS, MA_MATE, MA_SW = 0xFF00, 0x000F, 0x0030, 0x00C0
    rank = T.rank_of(core)
    if rank is None:
        if core % 8 == A_FOLD_CORE and (H(core), C(core)) in at:
            g.wait_ge(S.hAs, 16)
            fused([tr(cores[at[(H(core), C(core))]], T.mA[:, :], [T.hA[0], T.hA[1], T.hA[2], T.hA[3]], S.AA, 0xFFFF)])
            g.wait_ge(S.sent, sent[0])
        if core in a2_relay:
            g.wait_ge(S.a2r, _bits(M_SAME) + _bits(M_CROSS))
            masks = [0x0F, 0xF0]
            fused([tr(cd, T.a2l[j], [T.a2l[j]], S["a2a%d" % j], masks[n])
                   for n, (j, cd) in enumerate(a2_relay[core])])
            g.wait_ge(S.sent, sent[0])
        if core in g3_relay:
            t, k = g3_relay[core]
            g.wait_ge(S.g3r, 4)
            copy(root, T.g3l[k], T.g3s[t], S["g3a%d" % k])
            g.wait_ge(S.sent, sent[0])
        return

    h, ch = H(core), C(core)
    oc, sw, cb, dg = ch ^ 1, h ^ 1, 3 - h, (h + 2) % 4
    mate, swp, cbp = cores[at[(h, oc)]], cores[at[(sw, ch)]], cores[at[(cb, ch)]]

    def cols(hh, cc):
        a = 64 * G1.index(at[(hh, cc)])
        return T.x1[:, a:a + 64]

    slot_chunk = [(dg, oc), (cb, oc), (sw, oc), (h, oc), (dg, ch), (sw, ch), (cb, ch), (h, ch)]
    in2 = rank in G2
    fin = [0]

    def load(q, k):
        q.dma_start(T.xs[k], cols(*slot_chunk[k])).then_inc(S["L%d" % k], 16)

    def last(q, out, in_):
        q.dma_start(out, in_).then_inc(S.fin, 16)
        fin[0] += 16

    load(g.sync, 0)
    if in2:
        g.scalar.dma_start(T.a2s[:, :], T.x2[:, :]).then_inc(S.LX, 16)
    elif core in g3_first:
        g.scalar.dma_start(T.g3s[:, :, :], T.x3[:, :]).then_inc(S.LX, 16)
    load(g.scalar, 1)
    load(g.sync, 4)
    load(g.scalar, 2)
    load(g.sync, 3)
    load(g.scalar, 5)
    load(g.sync, 7)
    load(g.sync, 6)
    g.sync.wait_ge(S.AA, 16)
    g.sync.dma_start(T.y1[:, :], T.mA[:, :]).then_inc(S.yc, 16)

    if in2:
        i = G2.index(rank)
        last(g.scalar, T.y2[:, 2 * i:2 * i + 2], T.x2[:, 2 * i:2 * i + 2])
        far = []
        for j, rs in enumerate(G2):
            if j == i:
                continue
            if H(cores[rs]) == h:
                g.scalar.wait_ge(S["a2a%d" % j], _bits(M_DIRECT))
                last(g.scalar, T.y2[:, 2 * j:2 * j + 2], T.a2l[j, :, 2 * i:2 * i + 2])
            else:
                far.append(j)
        for q, j in zip([g.scalar, g.sync], far):
            q.wait_ge(S["a2a%d" % j], 4)
            last(q, T.y2[:, 2 * j:2 * j + 2], T.a2l[j, :, 2 * i:2 * i + 2])
    if core == root:
        last(g.scalar, T.y3[:, 256 * root3:256 * root3 + 256], T.x3[:, :])
        near = [j for j in g3_slot if H(cores[G3[j]]) == h]
        far = [j for j in g3_slot if H(cores[G3[j]]) != h]
        for t, q in enumerate([g.scalar, g.sync]):
            for j in near + far:
                q.wait_ge(S["g3a%d" % (g3_slot[j] + t)], 8)
                last(q, T.y3[64 * t:64 * t + 64, 256 * j:256 * j + 256], T.g3l[g3_slot[j] + t])

    g.wait_ge(S.L0, 16)
    copy(mate, T.m1[0], T.xs[0], S.A1a)
    if core in g3_first:
        g.wait_ge(S.LX, 16)
        fused([tr(tgt, T.g3s[t], [T.g3s[t]], S.g3r, m) for (tgt, t, m) in g3_first[core]])
    if in2:
        g.wait_ge(S.LX, 16)
        fused([tr(tgt, T.a2l[j], [T.a2s[:, :]], S.a2r if rel else S["a2a%d" % j], m)
               for (tgt, j, m, rel) in a2_out[core]])
    g.wait_ge(S.L1, 16)
    copy(mate, T.m1[1], T.xs[1], S.A1b)
    g.wait_ge(S.A1a, 8)
    g.wait_ge(S.L4, 16)
    fused([tr(swp, T.m2[:, :], [T.xs[4], T.m1[0]], S.A2, 0xFF)])
    for k in (2, 3, 5, 7):
        g.wait_ge(S["L%d" % k], 16)
    fused([tr(_wc(sw, oc, A_FOLD_CORE), T.hA[3], [T.xs[2]], S.hAs, MA_CROSS),
           tr(_wc(h, oc, A_FOLD_CORE), T.hA[1], [T.xs[3]], S.hAs, MA_MATE),
           tr(_wc(sw, ch, A_FOLD_CORE), T.hA[2], [T.xs[5]], S.hAs, MA_SW),
           tr(_wc(h, ch, A_FOLD_CORE), T.hA[0], [T.xs[7]], S.hAs, MA_ON)])
    g.wait_ge(S.A2, 8)
    g.wait_ge(S.A1b, 8)
    g.wait_ge(S.L6, 16)
    fused([tr(cbp, T.m3[:, :], [T.xs[6], T.m1[1], T.m2[:, :]], S.A3, 0xFF)])
    g.wait_ge(S.A3, 8)
    g.wait_ge(S.yc, 16)
    g.dma_start(T.y1[:, :], T.m3[:, :], accum_op=AluOpType.add, max_dma_last_dim=8192).then_inc(S.ysem, 16)
    g.wait_ge(S.ysem, 16)
    g.wait_ge(S.sent, sent[0])
    if fin[0]:
        g.wait_ge(S.fin, fin[0])
